import numpy as np
import ml_dtypes


def mxq(x, axis, fmt="e4m3"):
    dtype, down = {"e4m3": (ml_dtypes.float8_e4m3fn, 7), "e5m2": (ml_dtypes.float8_e5m2, 14)}[fmt]
    v = np.moveaxis(np.asarray(x, np.float32).astype(ml_dtypes.bfloat16).astype(np.float64), axis, -1)
    blocks = v.reshape(v.shape[:-1] + (-1, 32))
    amax = np.abs(blocks).max(-1, keepdims=True)
    byte = np.maximum(np.where(amax > 0, np.frexp(amax)[1] - 1 + 127, 0) - down, 1)
    scale = np.exp2(byte - 127.0)
    codes = (blocks / scale).astype(np.float32).astype(dtype).astype(np.float64)
    return np.moveaxis((codes * scale).reshape(v.shape), -1, axis)


WIDE = False


def mx_kscale(k):
    if not WIDE:
        return np.ones(k)
    levels = np.array([30, -30])
    if k % 512:
        return np.exp2(np.random.permutation(np.resize(levels, k // 32))).repeat(32)
    a = np.empty((k // 512, 16))
    for p in range(k // 512):
        a[p, :8] = np.random.permutation(np.resize(levels, 8))
        for g in range(8):
            far = levels[np.abs(levels - a[p, g]) >= 10]
            a[p, g + 8] = far[np.random.randint(len(far))]
    return np.exp2(a.ravel()).repeat(32)


def f64(x):
    return np.asarray(x).astype(np.float64)


def striped(idx):
    return np.tile(np.asarray(idx).reshape(-1, 16).T, (8, 1)).astype(np.uint16)


def unstriped(offs):
    return offs[:16].T.reshape(-1).astype(np.int64)


E2M1 = np.array([0.0, 0.5, 1.0, 1.5, 2.0, 3.0, 4.0, 6.0, -0.0, -0.5, -1.0, -1.5, -2.0, -3.0, -4.0, -6.0])


def pack_weight(w, fmt):
    k, n = w.shape
    w = f64(np.asarray(w, np.float32).astype(ml_dtypes.bfloat16)).reshape(k // 32, 32, n)
    amax = np.abs(w).max(1)
    if fmt in ("e4m3", "e5m2"):
        byte = np.frexp(amax)[1] - 1 + 127 - (7 if fmt == "e4m3" else 14)
    else:
        mant, ex = np.frexp(amax / 6.0)
        byte = np.where(mant > 0.5, ex, ex - 1) + 127
    byte = np.clip(np.where(amax > 0, byte, 1), 1, 254)
    scaled = (w * np.exp2(127.0 - byte)[:, None, :]).reshape(k, n).astype(np.float32)
    by_word = np.ascontiguousarray(scaled.reshape(k // 512, 128, 4, n).transpose(0, 1, 3, 2))
    if fmt in ("e4m3", "e5m2"):
        words = by_word.astype(ml_dtypes.float8_e4m3fn if fmt == "e4m3" else ml_dtypes.float8_e5m2).view(np.uint8)
    else:
        c = by_word.astype(ml_dtypes.float4_e2m1fn).view(np.uint8) & 0xF
        words = (c[..., 0::2] | (c[..., 1::2] << 4)).reshape(k // 512, 128, 2 * n)
    return np.ascontiguousarray(words), np.ascontiguousarray(byte.astype(np.uint8).reshape(k // 512, 16, n))


def unpack_weight(words, scales, fmt):
    g, _, n = scales.shape
    words = np.ascontiguousarray(words).reshape(g, 128, n, -1)
    if fmt in ("e4m3", "e5m2"):
        vals = words.view(ml_dtypes.float8_e4m3fn if fmt == "e4m3" else ml_dtypes.float8_e5m2).astype(np.float64)
    else:
        nib = np.empty((g, 128, n, 4), np.uint8)
        nib[..., 0::2] = words & 0xF
        nib[..., 1::2] = words >> 4
        vals = E2M1[nib]
    vals = vals * np.repeat(np.exp2(scales.astype(np.float64) - 127.0), 8, axis=1)[..., None]
    return vals.transpose(0, 1, 3, 2).reshape(g * 512, n)


K, T, J, R, O, N = 512, 512, 256, 512, 128, 256


def setup_inputs():
    n = np.random.standard_normal
    idx = np.random.permutation(T)[:J]
    idx2 = np.random.permutation(T)[:J]
    idx3 = np.random.permutation(J)[:O]
    idx4 = np.random.permutation(J)[:O]
    fk = mx_kscale(K)
    fr = mx_kscale(R)
    wp = pack_weight(n((K, R)) * 1 / np.sqrt(K) * fk[:, None] * fr, "e2m1")
    wbp = pack_weight(n((R, N)) * 1 / np.sqrt(R) / fr[:, None], "e5m2")
    return {
        "xf": (n((K, T))).astype(np.float32),
        "fk": (np.random.uniform(0.5, 2.0, (K, 1)) / fk[:, None]).astype(np.float32),
        "w_words": wp[0],
        "w_scales": wp[1],
        "wb_words": wbp[0],
        "wb_scales": wbp[1],
        "rs": (n((N, O))).astype(np.float32),
        "offs": striped(idx),
        "offs2": striped(idx2),
        "offs3": striped(idx3),
        "offs4": striped(idx4),
    }


def reference(xf, fk, w_words, w_scales, wb_words, wb_scales, rs, offs, offs2, offs3, offs4):
    idx = unstriped(offs)
    idx2 = unstriped(offs2)
    idx3 = unstriped(offs3)
    idx4 = unstriped(offs4)
    wu = unpack_weight(w_words, w_scales, "e2m1")
    wbu = unpack_weight(wb_words, wb_scales, "e5m2")
    u = np.maximum(f64(xf)[:, idx], f64(xf)[:, idx2]) * f64(fk)
    uq = mxq(u, 0, "e4m3")
    a = wu.T @ uq
    hid = np.abs(a[:, idx3] - 0.5 * a[:, idx4])
    hidq = mxq(hid, 0, "e5m2")
    p = wbu.T @ hidq
    p1 = np.pad(p, ((0, 0), (1, 0)))[:, :O]
    y = p - 0.7 * p1 + 0.5 * f64(rs)
    return y

@@ -1,0 +1,198 @@
+from contextlib import ExitStack
+
+import concourse.mybir as mybir
+
+K, T, J, R, O, N = 512, 512, 256, 512, 128, 256
+FLOPS = 2 * K * R * J + 2 * R * N * O
+
+F32 = mybir.dt.float32
+BF16 = mybir.dt.bfloat16
+I32 = mybir.dt.int32
+U32 = mybir.dt.uint32
+U16 = mybir.dt.uint16
+U8 = mybir.dt.uint8
+E4M3X4 = mybir.dt.float8_e4m3fn_x4
+E5M2X4 = mybir.dt.float8_e5m2_x4
+E2M1X4 = mybir.dt.float4_e2m1fn_x4
+ALU = mybir.AluOpType
+ACT = mybir.ActivationFunctionType
+
+P = 128
+PACK = 4
+HALF = J // 2
+
+
+def load_scale_rows(queue, plane, scales):
+    for quad in range(4):
+        queue.dma_start(
+            out=plane[32 * quad : 32 * quad + 4, :].bitcast(I32),
+            in_=scales[0, 4 * quad : 4 * quad + 4, :].bitcast(I32),
+        )
+
+
+def tile_list_looks_largerpicks_farther_lagged_kernel(
+    tc, xf, fk, w_words, w_scales, wb_words, wb_scales, rs, offs, offs2, offs3, offs4, out
+):
+    nc = tc.nc
+    with ExitStack() as ctx:
+        sb = ctx.enter_context(tc.tile_pool(name="sb", bufs=1))
+        ps = ctx.enter_context(tc.psum_pool(name="ps", bufs=1))
+
+        lists = [sb.tile([P, n // 16], U16, name="list%d" % i) for i, n in enumerate((J, J, O, O))]
+        x = [sb.tile([P, T], F32, name="x%d" % t) for t in range(PACK)]
+        x_rows = xf.rearrange("(p t) c -> p t c", t=PACK)
+        f = sb.tile([P, PACK], F32)
+        w_raw = sb.tile([P, 2 * R], U8)
+        ws_raw = sb.tile([P, R], U8, tag="reused", align_bytes=64)
+        wb = sb.tile([P, N], U32, align_bytes=64)
+        wbs = sb.tile([P, N], U8, align_bytes=64)
+        res = sb.tile([P, 2, O], F32)
+
+        nc.gpsimd.memset(ws_raw[:].bitcast(I32), 0)
+        nc.gpsimd.memset(wbs[:].bitcast(I32), 0)
+        nc.sync.dma_start(out=x[0][:], in_=x_rows[:, 0, :])
+        nc.sync.dma_start(lists[0][:], offs)
+        nc.sync.dma_start(lists[1][:], offs2)
+        for t in range(1, PACK - 1):
+            nc.sync.dma_start(out=x[t][:], in_=x_rows[:, t, :])
+        nc.sync.dma_start(out=w_raw[:].bitcast(I32), in_=w_words[0].bitcast(I32))
+        nc.sync.dma_start(out=x[3][:], in_=x_rows[:, 3, :])
+        nc.sync.dma_start(out=f[:], in_=fk.rearrange("(p t) o -> p (t o)", t=PACK))
+        load_scale_rows(nc.sync, ws_raw, w_scales)
+        nc.sync.dma_start(lists[2][:], offs3)
+        nc.sync.dma_start(lists[3][:], offs4)
+        nc.sync.dma_start(out=wb[:].bitcast(I32), in_=wb_words[0].rearrange("p n t -> p (n t)").bitcast(I32))
+        nc.sync.dma_start(out=res[:], in_=rs.rearrange("(h p) o -> p h o", p=P))
+        load_scale_rows(nc.sync, wbs, wb_scales)
+
+        first = sb.tile([P, PACK, J], F32)
+        second = sb.tile([P, PACK, J], F32)
+        larger = sb.tile([P, 2 * PACK - 1, HALF], F32)
+        EARLY, LATE = 1, 0
+
+        def cols(h):
+            return slice(h * HALF, (h + 1) * HALF)
+
+        def list_cols(h):
+            return slice(h * HALF // 16, (h + 1) * HALF // 16)
+
+        def keep_larger(t):
+            nc.vector.tensor_tensor(
+                larger[:, t : t + PACK : PACK - 1, :],
+                first[:, t, :].rearrange("p (h j) -> p h j", h=2),
+                second[:, t, :].rearrange("p (h j) -> p h j", h=2),
+                ALU.max,
+            )
+
+        def keep_larger_half(t, h):
+            nc.vector.tensor_tensor(larger[:, t + (PACK - 1) * h, :], first[:, t, cols(h)], second[:, t, cols(h)], ALU.max)
+
+        uq = [sb.tile([P, HALF], U32, name="uq%d" % h, align_bytes=64) for h in range(2)]
+        us = [sb.tile([P, HALF], U8, name="us%d" % h, align_bytes=64) for h in range(2)]
+
+        def scale_round(u, h):
+            s0 = (PACK - 1) * h
+            nc.vector.tensor_tensor(
+                u[:].rearrange("p (c i) t -> p c t i", i=4),
+                larger[:, s0 : s0 + PACK, :].rearrange("p t (c i) -> p c t i", i=4),
+                f[:].unsqueeze(1).unsqueeze(3).to_broadcast([P, HALF // 4, PACK, 4]),
+                ALU.mult,
+            )
+
+        def quantise(u, h):
+            nc.vector.quantize_mx(out=uq[h][:].bitcast(E4M3X4), scales=us[h][:], in_=u[:].rearrange("p c t -> p (c t)"))
+
+        w = sb.tile([P, 2 * R], U8, align_bytes=64)
+        ws = sb.tile([P, R], U8, align_bytes=64)
+        for t in range(2):
+            nc.vector.tensor_copy(first[:, t, :], x[t][:].indirect(lists[0][:]))
+            nc.scalar.activation(second[:, t, :], x[t][:].indirect(lists[1][:]), ACT.Copy)
+            keep_larger(t)
+        nc.scalar.activation(first[:, 2, :], x[2][:].indirect(lists[0][:]), ACT.Copy)
+        nc.scalar.activation(second[:, 2, :], x[2][:].indirect(lists[1][:]), ACT.Copy)
+        nc.vector.tensor_copy(
+            w[:].bitcast(U16).rearrange("p (t m) -> p t m", t=PACK),
+            w_raw[:].bitcast(U16).rearrange("p (m t) -> p t m", t=PACK),
+        )
+        nc.vector.tensor_copy(first[:, 3, cols(EARLY)], x[3][:].indirect(lists[0][:, list_cols(EARLY)]))
+        nc.scalar.activation(second[:, 3, cols(EARLY)], x[3][:].indirect(lists[1][:, list_cols(EARLY)]), ACT.Copy)
+        nc.scalar.activation(first[:, 3, cols(LATE)], x[3][:].indirect(lists[0][:, list_cols(LATE)]), ACT.Copy)
+        nc.scalar.activation(second[:, 3, cols(LATE)], x[3][:].indirect(lists[1][:, list_cols(LATE)]), ACT.Copy)
+        keep_larger(2)
+        keep_larger_half(3, EARLY)
+        u_early = sb.tile([P, HALF, PACK], BF16, align_bytes=64)
+        scale_round(u_early, EARLY)
+        keep_larger_half(3, LATE)
+        nc.vector.tensor_copy(
+            ws[:].rearrange("p (t m) -> p t m", t=PACK),
+            ws_raw[:].rearrange("p (m t) -> p t m", t=PACK),
+        )
+        quantise(u_early, EARLY)
+        u_late = sb.tile([P, HALF, PACK], BF16, tag="reused", align_bytes=64)
+        scale_round(u_late, LATE)
+        quantise(u_late, LATE)
+
+        a = [sb.tile([P, J], F32, name="a%d" % t) for t in range(PACK)]
+
+        def first_product(bank, t, h):
+            nc.tensor.matmul_mx(
+                out=bank,
+                lhsT=w[:, 2 * P * t : 2 * P * (t + 1)].bitcast(E2M1X4),
+                lhsT_scale=ws[:, P * t : P * (t + 1)],
+                rhs=uq[h][:].bitcast(E4M3X4),
+                rhs_scale=us[h][:],
+                start=True,
+                stop=True,
+            )
+
+        early = ps.tile([P, PACK, HALF], F32)
+        for t in range(PACK):
+            first_product(early[:, t, :], t, EARLY)
+        for t in range(PACK):
+            nc.scalar.activation(a[t][:, cols(EARLY)], early[:, t, :], ACT.Copy)
+
+        late = [ps.tile([P, HALF], F32, name="late%d" % t) for t in range(PACK)]
+        for t in range(PACK):
+            first_product(late[t][:], t, LATE)
+        halved = sb.tile([P, PACK, O], F32)
+        diff = sb.tile([P, PACK, O], F32)
+        for t in range(PACK):
+            if t == 1:
+                nc.scalar.activation(a[t][:, cols(LATE)], late[t][:], ACT.Copy)
+            else:
+                nc.vector.tensor_copy(a[t][:, cols(LATE)], late[t][:])
+        for t in range(PACK):
+            nc.scalar.activation(halved[:, t, :], a[t][:].indirect(lists[3][:]), ACT.Copy, scale=-0.5)
+            nc.vector.tensor_tensor(diff[:, t, :], a[t][:].indirect(lists[2][:]), halved[:, t, :], ALU.add)
+
+        hid = sb.tile([P, O, PACK], BF16, align_bytes=64)
+        for ts, cs in ((slice(0, 2), slice(0, O)), (slice(2, 4), slice(0, O // 2))):
+            nc.scalar.activation(
+                hid[:, cs, ts].rearrange("p (c i) t -> p c t i", i=4),
+                diff[:, ts, cs].rearrange("p t (c i) -> p c t i", i=4),
+                ACT.Abs,
+            )
+        rest = diff[:, 2:4, O // 2 :].rearrange("p t o -> p o t")
+        nc.vector.scalar_tensor_tensor(hid[:, O // 2 :, 2:4], rest, -1.0, rest, ALU.mult, ALU.max)
+        hq = sb.tile([P, O], U32, align_bytes=64)
+        hs = sb.tile([P, O], U8, align_bytes=64)
+        nc.vector.quantize_mx(out=hq[:].bitcast(E5M2X4), scales=hs[:], in_=hid[:].rearrange("p c t -> p (c t)"))
+
+        prod = [ps.tile([P, O], F32, name="prod%d" % h) for h in range(2)]
+        y = [sb.tile([P, O], F32, name="y%d" % h) for h in range(2)]
+        for h in range(2):
+            nc.tensor.matmul_mx(
+                out=prod[h][:],
+                lhsT=wb[:, P * h : P * (h + 1)].bitcast(E5M2X4),
+                lhsT_scale=wbs[:, P * h : P * (h + 1)],
+                rhs=hq[:].bitcast(E5M2X4),
+                rhs_scale=hs[:],
+                start=True,
+                stop=True,
+            )
+        for h in range(2):
+            nc.vector.scalar_tensor_tensor(y[h][:], res[:, h, :], 0.5, prod[h][:], ALU.mult, ALU.add)
+        for h in range(2):
+            nc.vector.scalar_tensor_tensor(y[h][:, 1:], prod[h][:, : O - 1], -0.7, y[h][:, 1:], ALU.mult, ALU.add)
+        nc.sync.dma_start(out=out[0:P, :], in_=y[0][:])
+        nc.scalar.dma_start(out=out[P : 2 * P, :], in_=y[1][:])

@@ -43,94 +43,103 @@ def tile_list_looks_largerpicks_farther_lagged_kernel(
         x_rows = xf.rearrange("(p t) c -> p t c", t=PACK)
         f = sb.tile([P, PACK], F32)
         w_raw = sb.tile([P, 2 * R], U8)
-        ws_raw = sb.tile([P, R], U8, tag="reused", align_bytes=64)
+        ws_raw = sb.tile([P, R], U8)
         wb = sb.tile([P, N], U32, align_bytes=64)
         wbs = sb.tile([P, N], U8, align_bytes=64)
         res = sb.tile([P, 2, O], F32)
 
-        nc.gpsimd.memset(ws_raw[:].bitcast(I32), 0)
-        nc.gpsimd.memset(wbs[:].bitcast(I32), 0)
+        nc.vector.memset(ws_raw[:].bitcast(I32), 0)
+        nc.vector.memset(wbs[:].bitcast(I32), 0)
         nc.sync.dma_start(out=x[0][:], in_=x_rows[:, 0, :])
         nc.sync.dma_start(lists[0][:], offs)
         nc.sync.dma_start(lists[1][:], offs2)
+        nc.sync.dma_start(out=w_raw[:].bitcast(I32), in_=w_words[0].bitcast(I32))
         for t in range(1, PACK - 1):
             nc.sync.dma_start(out=x[t][:], in_=x_rows[:, t, :])
-        nc.sync.dma_start(out=w_raw[:].bitcast(I32), in_=w_words[0].bitcast(I32))
+        load_scale_rows(nc.sync, ws_raw, w_scales)
         nc.sync.dma_start(out=x[3][:], in_=x_rows[:, 3, :])
         nc.sync.dma_start(out=f[:], in_=fk.rearrange("(p t) o -> p (t o)", t=PACK))
-        load_scale_rows(nc.sync, ws_raw, w_scales)
         nc.sync.dma_start(lists[2][:], offs3)
         nc.sync.dma_start(lists[3][:], offs4)
         nc.sync.dma_start(out=wb[:].bitcast(I32), in_=wb_words[0].rearrange("p n t -> p (n t)").bitcast(I32))
         nc.sync.dma_start(out=res[:], in_=rs.rearrange("(h p) o -> p h o", p=P))
         load_scale_rows(nc.sync, wbs, wb_scales)
 
+        warm = sb.tile([P, 2], F32)
+        nc.vector.memset(warm[:, 0:1], 0.0)
+        nc.scalar.activation(warm[:, 1:2], warm[:, 0:1], ACT.Abs)
         first = sb.tile([P, PACK, J], F32)
         second = sb.tile([P, PACK, J], F32)
-        larger = sb.tile([P, 2 * PACK - 1, HALF], F32)
+        larger = sb.tile([P, 2, PACK, HALF], F32)
         EARLY, LATE = 1, 0
 
         def cols(h):
             return slice(h * HALF, (h + 1) * HALF)
 
-        def list_cols(h):
-            return slice(h * HALF // 16, (h + 1) * HALF // 16)
+        def pick(engine, which, t, halves):
+            c = slice(min(halves) * HALF, (max(halves) + 1) * HALF)
+            picked = x[t][:].indirect(lists[which][:, c.start // 16 : c.stop // 16])
+            dst = (first, second)[which][:, t, c]
+            if (which, t, halves) == (0, 3, (EARLY,)):
+                dst = larger[:, LATE, 3, :]
+            if engine == "v":
+                nc.vector.tensor_copy(dst, picked)
+            else:
+                nc.scalar.activation(dst, picked, ACT.Copy)
 
-        def keep_larger(t):
+        def keep_larger(ts):
             nc.vector.tensor_tensor(
-                larger[:, t : t + PACK : PACK - 1, :],
-                first[:, t, :].rearrange("p (h j) -> p h j", h=2),
-                second[:, t, :].rearrange("p (h j) -> p h j", h=2),
+                larger[:, :, ts, :].rearrange("p h t j -> p t h j"),
+                first[:, ts, :].rearrange("p t (h j) -> p t h j", h=2),
+                second[:, ts, :].rearrange("p t (h j) -> p t h j", h=2),
                 ALU.max,
             )
 
-        def keep_larger_half(t, h):
-            nc.vector.tensor_tensor(larger[:, t + (PACK - 1) * h, :], first[:, t, cols(h)], second[:, t, cols(h)], ALU.max)
-
         uq = [sb.tile([P, HALF], U32, name="uq%d" % h, align_bytes=64) for h in range(2)]
         us = [sb.tile([P, HALF], U8, name="us%d" % h, align_bytes=64) for h in range(2)]
-
-        def scale_round(u, h):
-            s0 = (PACK - 1) * h
-            nc.vector.tensor_tensor(
-                u[:].rearrange("p (c i) t -> p c t i", i=4),
-                larger[:, s0 : s0 + PACK, :].rearrange("p t (c i) -> p c t i", i=4),
-                f[:].unsqueeze(1).unsqueeze(3).to_broadcast([P, HALF // 4, PACK, 4]),
-                ALU.mult,
-            )
 
         def quantise(u, h):
             nc.vector.quantize_mx(out=uq[h][:].bitcast(E4M3X4), scales=us[h][:], in_=u[:].rearrange("p c t -> p (c t)"))
 
         w = sb.tile([P, 2 * R], U8, align_bytes=64)
         ws = sb.tile([P, R], U8, align_bytes=64)
-        for t in range(2):
-            nc.vector.tensor_copy(first[:, t, :], x[t][:].indirect(lists[0][:]))
-            nc.scalar.activation(second[:, t, :], x[t][:].indirect(lists[1][:]), ACT.Copy)
-            keep_larger(t)
-        nc.scalar.activation(first[:, 2, :], x[2][:].indirect(lists[0][:]), ACT.Copy)
-        nc.scalar.activation(second[:, 2, :], x[2][:].indirect(lists[1][:]), ACT.Copy)
+        BOTH = (EARLY, LATE)
+        pick("v", 0, 0, BOTH)
+        pick("s", 1, 0, BOTH)
+        pick("v", 0, 1, BOTH)
+        pick("s", 1, 1, BOTH)
+        pick("v", 0, 2, (EARLY,))
+        keep_larger(slice(0, 2))
+        pick("s", 1, 2, BOTH)
+        pick("s", 0, 2, (LATE,))
+        for h in BOTH:
+            pick("s", 0, 3, (h,))
+            pick("s", 1, 3, (h,))
         nc.vector.tensor_copy(
             w[:].bitcast(U16).rearrange("p (t m) -> p t m", t=PACK),
             w_raw[:].bitcast(U16).rearrange("p (m t) -> p t m", t=PACK),
         )
-        nc.vector.tensor_copy(first[:, 3, cols(EARLY)], x[3][:].indirect(lists[0][:, list_cols(EARLY)]))
-        nc.scalar.activation(second[:, 3, cols(EARLY)], x[3][:].indirect(lists[1][:, list_cols(EARLY)]), ACT.Copy)
-        nc.scalar.activation(first[:, 3, cols(LATE)], x[3][:].indirect(lists[0][:, list_cols(LATE)]), ACT.Copy)
-        nc.scalar.activation(second[:, 3, cols(LATE)], x[3][:].indirect(lists[1][:, list_cols(LATE)]), ACT.Copy)
-        keep_larger(2)
-        keep_larger_half(3, EARLY)
-        u_early = sb.tile([P, HALF, PACK], BF16, align_bytes=64)
-        scale_round(u_early, EARLY)
-        keep_larger_half(3, LATE)
+        keep_larger(slice(2, 3))
         nc.vector.tensor_copy(
             ws[:].rearrange("p (t m) -> p t m", t=PACK),
             ws_raw[:].rearrange("p (m t) -> p t m", t=PACK),
         )
-        quantise(u_early, EARLY)
-        u_late = sb.tile([P, HALF, PACK], BF16, tag="reused", align_bytes=64)
-        scale_round(u_late, LATE)
-        quantise(u_late, LATE)
+        u = [sb.tile([P, HALF, PACK], BF16, name="u%d" % h, align_bytes=64) for h in range(2)]
+
+        def scale_round(h):
+            nc.vector.tensor_tensor(
+                u[h][:].rearrange("p (c i) t -> p c t i", i=4),
+                larger[:, h].rearrange("p t (c i) -> p c t i", i=4),
+                f[:].unsqueeze(1).unsqueeze(3).to_broadcast([P, HALF // 4, PACK, 4]),
+                ALU.mult,
+            )
+
+        nc.vector.tensor_tensor(larger[:, EARLY, 3, :], larger[:, LATE, 3, :], second[:, 3, cols(EARLY)], ALU.max)
+        scale_round(EARLY)
+        nc.vector.tensor_tensor(larger[:, LATE, 3, :], first[:, 3, cols(LATE)], second[:, 3, cols(LATE)], ALU.max)
+        quantise(u[EARLY], EARLY)
+        scale_round(LATE)
+        quantise(u[LATE], LATE)
 
         a = [sb.tile([P, J], F32, name="a%d" % t) for t in range(PACK)]
 
@@ -145,11 +154,11 @@ def tile_list_looks_largerpicks_farther_lagged_kernel(
                 stop=True,
             )
 
-        early = ps.tile([P, PACK, HALF], F32)
+        early = [ps.tile([P, HALF], F32, name="early%d" % t, tag="bank%d" % t) for t in range(PACK)]
         for t in range(PACK):
-            first_product(early[:, t, :], t, EARLY)
+            first_product(early[t][:], t, EARLY)
         for t in range(PACK):
-            nc.scalar.activation(a[t][:, cols(EARLY)], early[:, t, :], ACT.Copy)
+            nc.scalar.activation(a[t][:, cols(EARLY)], early[t][:], ACT.Copy)
 
         late = [ps.tile([P, HALF], F32, name="late%d" % t) for t in range(PACK)]
         for t in range(PACK):
@@ -178,7 +187,7 @@ def tile_list_looks_largerpicks_farther_lagged_kernel(
         hs = sb.tile([P, O], U8, align_bytes=64)
         nc.vector.quantize_mx(out=hq[:].bitcast(E5M2X4), scales=hs[:], in_=hid[:].rearrange("p c t -> p (c t)"))
 
-        prod = [ps.tile([P, O], F32, name="prod%d" % h) for h in range(2)]
+        prod = [ps.tile([P, O], F32, name="prod%d" % h, tag="bank%d" % h) for h in range(2)]
         y = [sb.tile([P, O], F32, name="y%d" % h) for h in range(2)]
         for h in range(2):
             nc.tensor.matmul_mx(

@@ -20,6 +20,7 @@ ACT = mybir.ActivationFunctionType
 P = 128
 PACK = 4
 HALF = J // 2
+SHARE = 96
 
 
 def load_scale_rows(queue, plane, scales):
@@ -126,19 +127,21 @@ def tile_list_looks_largerpicks_farther_lagged_kernel(
         )
         u = [sb.tile([P, HALF, PACK], BF16, name="u%d" % h, align_bytes=64) for h in range(2)]
 
-        def scale_round(h):
+        def scale_round(h, c0):
             nc.vector.tensor_tensor(
-                u[h][:].rearrange("p (c i) t -> p c t i", i=4),
-                larger[:, h].rearrange("p t (c i) -> p c t i", i=4),
-                f[:].unsqueeze(1).unsqueeze(3).to_broadcast([P, HALF // 4, PACK, 4]),
+                u[h][:, c0:, :].rearrange("p (c i) t -> p c t i", i=4),
+                larger[:, h, :, c0:].rearrange("p t (c i) -> p c t i", i=4),
+                f[:].unsqueeze(1).unsqueeze(3).to_broadcast([P, (HALF - c0) // 4, PACK, 4]),
                 ALU.mult,
             )
 
         nc.vector.tensor_tensor(larger[:, EARLY, 3, :], larger[:, LATE, 3, :], second[:, 3, cols(EARLY)], ALU.max)
-        scale_round(EARLY)
+        scale_round(EARLY, 0)
         nc.vector.tensor_tensor(larger[:, LATE, 3, :], first[:, 3, cols(LATE)], second[:, 3, cols(LATE)], ALU.max)
         quantise(u[EARLY], EARLY)
-        scale_round(LATE)
+        for t in range(PACK):
+            nc.scalar.activation(u[LATE][:, :SHARE, t], larger[:, LATE, t, :SHARE], ACT.Copy, scale=f[:, t : t + 1])
+        scale_round(LATE, SHARE)
         quantise(u[LATE], LATE)
 
         a = [sb.tile([P, J], F32, name="a%d" % t) for t in range(PACK)]

from contextlib import ExitStack

import concourse.mybir as mybir

K, T, J, R, O, N = 512, 512, 256, 512, 128, 256
FLOPS = 2 * K * R * J + 2 * R * N * O

F32 = mybir.dt.float32
BF16 = mybir.dt.bfloat16
I32 = mybir.dt.int32
U32 = mybir.dt.uint32
U16 = mybir.dt.uint16
U8 = mybir.dt.uint8
E4M3X4 = mybir.dt.float8_e4m3fn_x4
E5M2X4 = mybir.dt.float8_e5m2_x4
E2M1X4 = mybir.dt.float4_e2m1fn_x4
ALU = mybir.AluOpType
ACT = mybir.ActivationFunctionType

P = 128
PACK = 4
HALF = J // 2
SHARE = 96


def load_scale_rows(queue, plane, scales):
    for quad in range(4):
        queue.dma_start(
            out=plane[32 * quad : 32 * quad + 4, :].bitcast(I32),
            in_=scales[0, 4 * quad : 4 * quad + 4, :].bitcast(I32),
        )


def tile_list_looks_largerpicks_farther_lagged_kernel(
    tc, xf, fk, w_words, w_scales, wb_words, wb_scales, rs, offs, offs2, offs3, offs4, out
):
    nc = tc.nc
    with ExitStack() as ctx:
        sb = ctx.enter_context(tc.tile_pool(name="sb", bufs=1))
        ps = ctx.enter_context(tc.psum_pool(name="ps", bufs=1))

        lists = [sb.tile([P, n // 16], U16, name="list%d" % i) for i, n in enumerate((J, J, O, O))]
        x = [sb.tile([P, T], F32, name="x%d" % t) for t in range(PACK)]
        x_rows = xf.rearrange("(p t) c -> p t c", t=PACK)
        f = sb.tile([P, PACK], F32)
        w_raw = sb.tile([P, 2 * R], U8)
        ws_raw = sb.tile([P, R], U8)
        wb = sb.tile([P, N], U32, align_bytes=64)
        wbs = sb.tile([P, N], U8, align_bytes=64)
        res = sb.tile([P, 2, O], F32)

        nc.vector.memset(ws_raw[:].bitcast(I32), 0)
        nc.vector.memset(wbs[:].bitcast(I32), 0)
        nc.sync.dma_start(out=x[0][:], in_=x_rows[:, 0, :])
        nc.sync.dma_start(lists[0][:], offs)
        nc.sync.dma_start(lists[1][:], offs2)
        nc.sync.dma_start(out=w_raw[:].bitcast(I32), in_=w_words[0].bitcast(I32))
        for t in range(1, PACK - 1):
            nc.sync.dma_start(out=x[t][:], in_=x_rows[:, t, :])
        load_scale_rows(nc.sync, ws_raw, w_scales)
        nc.sync.dma_start(out=x[3][:], in_=x_rows[:, 3, :])
        nc.sync.dma_start(out=f[:], in_=fk.rearrange("(p t) o -> p (t o)", t=PACK))
        nc.sync.dma_start(lists[2][:], offs3)
        nc.sync.dma_start(lists[3][:], offs4)
        nc.sync.dma_start(out=wb[:].bitcast(I32), in_=wb_words[0].rearrange("p n t -> p (n t)").bitcast(I32))
        nc.sync.dma_start(out=res[:], in_=rs.rearrange("(h p) o -> p h o", p=P))
        load_scale_rows(nc.sync, wbs, wb_scales)

        warm = sb.tile([P, 2], F32)
        nc.vector.memset(warm[:, 0:1], 0.0)
        nc.scalar.activation(warm[:, 1:2], warm[:, 0:1], ACT.Abs)
        first = sb.tile([P, PACK, J], F32)
        second = sb.tile([P, PACK, J], F32)
        larger = sb.tile([P, 2, PACK, HALF], F32)
        EARLY, LATE = 1, 0

        def cols(h):
            return slice(h * HALF, (h + 1) * HALF)

        def pick(engine, which, t, halves):
            c = slice(min(halves) * HALF, (max(halves) + 1) * HALF)
            picked = x[t][:].indirect(lists[which][:, c.start // 16 : c.stop // 16])
            dst = (first, second)[which][:, t, c]
            if (which, t, halves) == (0, 3, (EARLY,)):
                dst = larger[:, LATE, 3, :]
            if engine == "v":
                nc.vector.tensor_copy(dst, picked)
            else:
                nc.scalar.activation(dst, picked, ACT.Copy)

        def keep_larger(ts):
            nc.vector.tensor_tensor(
                larger[:, :, ts, :].rearrange("p h t j -> p t h j"),
                first[:, ts, :].rearrange("p t (h j) -> p t h j", h=2),
                second[:, ts, :].rearrange("p t (h j) -> p t h j", h=2),
                ALU.max,
            )

        uq = [sb.tile([P, HALF], U32, name="uq%d" % h, align_bytes=64) for h in range(2)]
        us = [sb.tile([P, HALF], U8, name="us%d" % h, align_bytes=64) for h in range(2)]

        def quantise(u, h):
            nc.vector.quantize_mx(out=uq[h][:].bitcast(E4M3X4), scales=us[h][:], in_=u[:].rearrange("p c t -> p (c t)"))

        w = sb.tile([P, 2 * R], U8, align_bytes=64)
        ws = sb.tile([P, R], U8, align_bytes=64)
        BOTH = (EARLY, LATE)
        pick("v", 0, 0, BOTH)
        pick("s", 1, 0, BOTH)
        pick("v", 0, 1, BOTH)
        pick("s", 1, 1, BOTH)
        pick("v", 0, 2, (EARLY,))
        keep_larger(slice(0, 2))
        pick("s", 1, 2, BOTH)
        pick("s", 0, 2, (LATE,))
        for h in BOTH:
            pick("s", 0, 3, (h,))
            pick("s", 1, 3, (h,))
        nc.vector.tensor_copy(
            w[:].bitcast(U16).rearrange("p (t m) -> p t m", t=PACK),
            w_raw[:].bitcast(U16).rearrange("p (m t) -> p t m", t=PACK),
        )
        keep_larger(slice(2, 3))
        nc.vector.tensor_copy(
            ws[:].rearrange("p (t m) -> p t m", t=PACK),
            ws_raw[:].rearrange("p (m t) -> p t m", t=PACK),
        )
        u = [sb.tile([P, HALF, PACK], BF16, name="u%d" % h, align_bytes=64) for h in range(2)]

        def scale_round(h, c0):
            nc.vector.tensor_tensor(
                u[h][:, c0:, :].rearrange("p (c i) t -> p c t i", i=4),
                larger[:, h, :, c0:].rearrange("p t (c i) -> p c t i", i=4),
                f[:].unsqueeze(1).unsqueeze(3).to_broadcast([P, (HALF - c0) // 4, PACK, 4]),
                ALU.mult,
            )

        nc.vector.tensor_tensor(larger[:, EARLY, 3, :], larger[:, LATE, 3, :], second[:, 3, cols(EARLY)], ALU.max)
        scale_round(EARLY, 0)
        nc.vector.tensor_tensor(larger[:, LATE, 3, :], first[:, 3, cols(LATE)], second[:, 3, cols(LATE)], ALU.max)
        quantise(u[EARLY], EARLY)
        for t in range(PACK):
            nc.scalar.activation(u[LATE][:, :SHARE, t], larger[:, LATE, t, :SHARE], ACT.Copy, scale=f[:, t : t + 1])
        scale_round(LATE, SHARE)
        quantise(u[LATE], LATE)

        a = [sb.tile([P, J], F32, name="a%d" % t) for t in range(PACK)]

        def first_product(bank, t, h):
            nc.tensor.matmul_mx(
                out=bank,
                lhsT=w[:, 2 * P * t : 2 * P * (t + 1)].bitcast(E2M1X4),
                lhsT_scale=ws[:, P * t : P * (t + 1)],
                rhs=uq[h][:].bitcast(E4M3X4),
                rhs_scale=us[h][:],
                start=True,
                stop=True,
            )

        early = [ps.tile([P, HALF], F32, name="early%d" % t, tag="bank%d" % t) for t in range(PACK)]
        for t in range(PACK):
            first_product(early[t][:], t, EARLY)
        for t in range(PACK):
            nc.scalar.activation(a[t][:, cols(EARLY)], early[t][:], ACT.Copy)

        late = [ps.tile([P, HALF], F32, name="late%d" % t) for t in range(PACK)]
        for t in range(PACK):
            first_product(late[t][:], t, LATE)
        halved = sb.tile([P, PACK, O], F32)
        diff = sb.tile([P, PACK, O], F32)
        for t in range(PACK):
            if t == 1:
                nc.scalar.activation(a[t][:, cols(LATE)], late[t][:], ACT.Copy)
            else:
                nc.vector.tensor_copy(a[t][:, cols(LATE)], late[t][:])
        for t in range(PACK):
            nc.scalar.activation(halved[:, t, :], a[t][:].indirect(lists[3][:]), ACT.Copy, scale=-0.5)
            nc.vector.tensor_tensor(diff[:, t, :], a[t][:].indirect(lists[2][:]), halved[:, t, :], ALU.add)

        hid = sb.tile([P, O, PACK], BF16, align_bytes=64)
        for ts, cs in ((slice(0, 2), slice(0, O)), (slice(2, 4), slice(0, O // 2))):
            nc.scalar.activation(
                hid[:, cs, ts].rearrange("p (c i) t -> p c t i", i=4),
                diff[:, ts, cs].rearrange("p t (c i) -> p c t i", i=4),
                ACT.Abs,
            )
        rest = diff[:, 2:4, O // 2 :].rearrange("p t o -> p o t")
        nc.vector.scalar_tensor_tensor(hid[:, O // 2 :, 2:4], rest, -1.0, rest, ALU.mult, ALU.max)
        hq = sb.tile([P, O], U32, align_bytes=64)
        hs = sb.tile([P, O], U8, align_bytes=64)
        nc.vector.quantize_mx(out=hq[:].bitcast(E5M2X4), scales=hs[:], in_=hid[:].rearrange("p c t -> p (c t)"))

        prod = [ps.tile([P, O], F32, name="prod%d" % h, tag="bank%d" % h) for h in range(2)]
        y = [sb.tile([P, O], F32, name="y%d" % h) for h in range(2)]
        for h in range(2):
            nc.tensor.matmul_mx(
                out=prod[h][:],
                lhsT=wb[:, P * h : P * (h + 1)].bitcast(E5M2X4),
                lhsT_scale=wbs[:, P * h : P * (h + 1)],
                rhs=hq[:].bitcast(E5M2X4),
                rhs_scale=hs[:],
                start=True,
                stop=True,
            )
        for h in range(2):
            nc.vector.scalar_tensor_tensor(y[h][:], res[:, h, :], 0.5, prod[h][:], ALU.mult, ALU.add)
        for h in range(2):
            nc.vector.scalar_tensor_tensor(y[h][:, 1:], prod[h][:, : O - 1], -0.7, y[h][:, 1:], ALU.mult, ALU.add)
        nc.sync.dma_start(out=out[0:P, :], in_=y[0][:])
        nc.scalar.dma_start(out=out[P : 2 * P, :], in_=y[1][:])
